import numpy as np
import ml_dtypes


def mxq(x, axis, fmt="e4m3"):
    dtype, down = {"e4m3": (ml_dtypes.float8_e4m3fn, 7), "e5m2": (ml_dtypes.float8_e5m2, 14)}[fmt]
    v = np.moveaxis(np.asarray(x, np.float32).astype(ml_dtypes.bfloat16).astype(np.float64), axis, -1)
    blocks = v.reshape(v.shape[:-1] + (-1, 32))
    amax = np.abs(blocks).max(-1, keepdims=True)
    byte = np.maximum(np.where(amax > 0, np.frexp(amax)[1] - 1 + 127, 0) - down, 1)
    scale = np.exp2(byte - 127.0)
    codes = (blocks / scale).astype(np.float32).astype(dtype).astype(np.float64)
    return np.moveaxis((codes * scale).reshape(v.shape), -1, axis)


WIDE = False


def mx_kscale(k):
    if not WIDE:
        return np.ones(k)
    levels = np.array([10, -10, 5, -5, 0])
    if k % 512:
        return np.exp2(np.random.permutation(np.resize(levels, k // 32))).repeat(32)
    a = np.empty((k // 512, 16))
    for p in range(k // 512):
        a[p, :8] = np.random.permutation(np.resize(levels, 8))
        for g in range(8):
            far = levels[np.abs(levels - a[p, g]) >= 10]
            a[p, g + 8] = far[np.random.randint(len(far))]
    return np.exp2(a.ravel()).repeat(32)


def f64(x):
    return np.asarray(x).astype(np.float64)


def striped(idx):
    return np.tile(idx.reshape(-1, 16).T, (8, 1)).astype(np.uint16)


def unstriped(offs):
    return offs[:16].T.reshape(-1).astype(np.int64)


def pack_weight(w):
    k, n = w.shape
    w = f64(np.asarray(w, np.float32).astype(ml_dtypes.bfloat16)).reshape(k // 32, 32, n)
    amax = np.abs(w).max(1)
    byte = np.clip(np.where(amax > 0, np.frexp(amax)[1] - 1 + 127 - 7, 1), 1, 254)
    scaled = (w * np.exp2(127.0 - byte)[:, None, :]).reshape(k, n).astype(np.float32)
    words = np.ascontiguousarray(scaled.reshape(k // 512, 128, 4, n).transpose(0, 1, 3, 2)).astype(ml_dtypes.float8_e4m3fn).view(np.uint8)
    return words, np.ascontiguousarray(byte.astype(np.uint8).reshape(k // 512, 16, n))


def unpack_weight(words, scales):
    g, p, n, _ = words.shape
    vals = np.ascontiguousarray(words).view(ml_dtypes.float8_e4m3fn).astype(np.float64) * np.repeat(np.exp2(scales.astype(np.float64) - 127.0), 8, axis=1)[..., None]
    return vals.transpose(0, 1, 3, 2).reshape(g * 512, n)


E2M1 = np.array([0.0, 0.5, 1.0, 1.5, 2.0, 3.0, 4.0, 6.0, -0.0, -0.5, -1.0, -1.5, -2.0, -3.0, -4.0, -6.0])


def pack_fp4(w):
    k, n = w.shape
    w = f64(np.asarray(w, np.float32).astype(ml_dtypes.bfloat16)).reshape(k // 32, 32, n)
    amax = np.abs(w).max(1)
    mant, ex = np.frexp(amax / 6.0)
    byte = np.clip(np.where(amax > 0, np.where(mant > 0.5, ex, ex - 1) + 127, 1), 1, 254)
    scaled = (w * np.exp2(127.0 - byte)[:, None, :]).reshape(k, n).astype(np.float32)
    c = np.ascontiguousarray(scaled.reshape(k // 512, 128, 4, n).transpose(0, 1, 3, 2)).astype(ml_dtypes.float4_e2m1fn).view(np.uint8) & 0xF
    words = (c[..., 0::2] | (c[..., 1::2] << 4)).reshape(k // 512, 128, 2 * n)
    return np.ascontiguousarray(words), np.ascontiguousarray(byte.astype(np.uint8).reshape(k // 512, 16, n))


def unpack_fp4(words, scales):
    g, _, n = scales.shape
    words = np.ascontiguousarray(words).reshape(g, 128, n, 2)
    nib = np.empty((g, 128, n, 4), np.uint8)
    nib[..., 0::2] = words & 0xF
    nib[..., 1::2] = words >> 4
    vals = E2M1[nib] * np.repeat(np.exp2(scales.astype(np.float64) - 127.0), 8, axis=1)[..., None]
    return vals.transpose(0, 1, 3, 2).reshape(g * 512, n)


def relu(v):
    return np.maximum(v, 0.0)


K, T, S, D, V, H, N, U = 512, 2048, 1024, 3, 512, 512, 128, 256
P = 2 ** 7


def setup_inputs():
    n = np.random.standard_normal
    s = mx_kscale(K)[:, None]
    u = mx_kscale(H)
    packed_xT = pack_weight(n((K, T)) * s)
    packed_w2 = pack_fp4(n((H, N)) / np.sqrt(H) / u[:, None])
    return {
        "x_words": packed_xT[0],
        "x_scales": packed_xT[1],
        "w1": (n((K, H)) / np.sqrt(K) / s * u).astype(np.float32),
        "w2_words": packed_w2[0],
        "w2_scales": packed_w2[1],
        "gate": (np.tile(np.random.uniform(0.2, 1.0, (D, 1, V)) / np.sqrt(D), (1, P, 1))).astype(np.float32),
        "gate2": (np.tile(np.random.uniform(0.2, 1.0, (D, 1, U)) / np.sqrt(D), (1, P, 1))).astype(np.float32),
        "offs": striped(np.random.permutation(T)[:S]),
        "pos1": striped(np.random.permutation(S)[:V]),
        "pos2": striped(np.random.permutation(S)[:V]),
        "pos3": striped(np.random.permutation(S)[:V]),
        "nxt1": striped(np.random.permutation(V)[:U]),
        "nxt2": striped(np.random.permutation(V)[:U]),
        "nxt3": striped(np.random.permutation(V)[:U]),
    }


def reference(x_words, x_scales, w1, w2_words, w2_scales, gate, gate2, offs, pos1, pos2, pos3, nxt1, nxt2, nxt3):
    xq = unpack_weight(x_words, x_scales)[:, unstriped(offs)]
    h = relu(mxq(f64(w1), 0, "e4m3").T @ xq)
    z = h[:, unstriped(pos1)] * f64(gate)[0, :1] + h[:, unstriped(pos2)] * f64(gate)[1, :1] + h[:, unstriped(pos3)] * f64(gate)[2, :1]
    g = relu(unpack_fp4(w2_words, w2_scales).T @ mxq(z, 0, "e4m3"))
    return g[:, unstriped(nxt1)] * f64(gate2)[0, :1] + g[:, unstriped(nxt2)] * f64(gate2)[1, :1] + g[:, unstriped(nxt3)] * f64(gate2)[2, :1]

@@ -1,0 +1,205 @@
+from contextlib import ExitStack
+
+import concourse.mybir as mybir
+from concourse.masks import make_identity
+
+K, T, S, D, V, H, N, U = 512, 2048, 1024, 3, 512, 512, 128, 256
+FLOPS = 2 * K * H * S + 2 * H * N * V
+
+F32 = mybir.dt.float32
+BF16 = mybir.dt.bfloat16
+I32 = mybir.dt.int32
+U32 = mybir.dt.uint32
+U16 = mybir.dt.uint16
+U8 = mybir.dt.uint8
+FP8X4 = mybir.dt.float8_e4m3fn_x4
+FP4X4 = mybir.dt.float4_e2m1fn_x4
+MULT = mybir.AluOpType.mult
+ADD = mybir.AluOpType.add
+MAX = mybir.AluOpType.max
+RELU = mybir.ActivationFunctionType.Relu
+COPY = mybir.ActivationFunctionType.Copy
+
+P = 128
+PACK = 4
+LANES = 16
+TILES = H // P
+WORD_SLICES = ((0, 512), (512, 768), (768, 1024))
+W1_LOADS = ((0, 1), (1, 2), (2, 3), (3, 4))
+PIECES = ((0, 2), (2, 3), (3, 4))
+
+
+def tile_picked_hop2_relu_p_kernel(
+    tc, x_words, x_scales, w1, w2_words, w2_scales, gate, gate2, offs, pos1, pos2, pos3, nxt1, nxt2, nxt3, out
+):
+    nc = tc.nc
+    with ExitStack() as ctx:
+        keep = ctx.enter_context(tc.tile_pool(name="keep", bufs=1))
+        psum = ctx.enter_context(tc.psum_pool(name="psum", bufs=1))
+
+        def load_list(ap, name):
+            t = keep.tile(list(ap.shape), U16, name=name)
+            nc.sync.dma_start(t[:], ap)
+            return t
+
+        w1_rows = w1.rearrange("(p j) c -> p j c", j=PACK)
+        w1_raw = {}
+
+        def load_w1(t0, t1):
+            raw = keep.tile([P, PACK, (t1 - t0) * P], F32, name=f"w1_raw{t0}")
+            nc.sync.dma_start(raw[:], w1_rows[:, :, t0 * P : t1 * P])
+            for t in range(t0, t1):
+                w1_raw[t] = raw[:, :, (t - t0) * P : (t - t0 + 1) * P]
+
+        xs_all = keep.tile([P, T], U8, name="xs_all", align_bytes=64)
+        nc.vector.memset(xs_all[:].bitcast(I32), 0)
+        w2_s = keep.tile([P, N], U8, name="w2_s", align_bytes=64)
+        zeros = keep.tile([P, N // PACK], I32, name="zeros", tag="xw_all", align_bytes=64)
+        nc.vector.memset(zeros[:], 0)
+        nc.vector.tensor_copy(w2_s[:].bitcast(I32), zeros[:])
+        ident = keep.tile([P, P], F32, name="ident")
+        make_identity(nc, ident[:])
+
+        offs_t = load_list(offs, "offs_t")
+        load_w1(*W1_LOADS[0])
+        for q in range(4):
+            nc.sync.dma_start(xs_all[32 * q : 32 * q + 4, :].bitcast(I32), x_scales[0, 4 * q : 4 * q + 4, :].bitcast(I32))
+        xw_all = keep.tile([P, T], U32, name="xw_all", tag="xw_all", align_bytes=64)
+        nc.sync.dma_start(xw_all[:].bitcast(I32), x_words[0].rearrange("p c r -> p (c r)").bitcast(I32))
+        for t0, t1 in W1_LOADS[1:]:
+            load_w1(t0, t1)
+        pos_t = []
+        gate_t = []
+        for dd, ap in enumerate((pos1, pos2, pos3)):
+            pos_t.append(load_list(ap, f"pos_t{dd}"))
+            gt = keep.tile([P, V], F32, name=f"gate_t{dd}")
+            nc.sync.dma_start(gt[:], gate[dd])
+            gate_t.append(gt)
+        w2_w = keep.tile([P, 2 * N], U8, name="w2_w", align_bytes=64)
+        nc.sync.dma_start(w2_w[:].bitcast(I32), w2_words[0].bitcast(I32))
+        for q in range(4):
+            nc.sync.dma_start(w2_s[32 * q : 32 * q + 4, :].bitcast(I32), w2_scales[0, 4 * q : 4 * q + 4, :].bitcast(I32))
+        nxt_t = [load_list(ap, f"nxt_t{dd}") for dd, ap in enumerate((nxt1, nxt2, nxt3))]
+        gate2_t = keep.tile([P, D, U], F32, name="gate2_t")
+        nc.sync.dma_start(gate2_t[:], gate2.rearrange("d p r -> p d r"))
+
+        w1_codes = {}
+        w1_scales = {}
+
+        def quantize_w1(t):
+            grouped = keep.tile([P, P, PACK], BF16, name=f"w1_grouped{t}", align_bytes=64)
+            nc.scalar.activation(grouped[:], w1_raw[t].rearrange("p j c -> p c j"), COPY)
+            w1_codes[t] = keep.tile([P, P], U32, name=f"w1_codes{t}", align_bytes=64)
+            w1_scales[t] = keep.tile([P, P], U8, name=f"w1_scales{t}", align_bytes=64)
+            nc.vector.quantize_mx(
+                out=w1_codes[t][:].bitcast(FP8X4), scales=w1_scales[t][:], in_=grouped[:].rearrange("p c j -> p (c j)")
+            )
+
+        xs = keep.tile([P, S], U8, name="xs", align_bytes=64)
+        xw = keep.tile([P, S], U32, name="xw", align_bytes=64)
+        nc.vector.tensor_copy(xs[:], xs_all[:].indirect(offs_t[:]))
+        quantize_w1(0)
+
+        h = [keep.tile([P, S], F32, name=f"h{t}") for t in range(TILES)]
+
+        def first_product(t, a, b):
+            acc = psum.tile([P, b - a], F32, name="acc", tag="acc", bufs=4)
+            nc.tensor.matmul_mx(
+                out=acc[:],
+                lhsT=w1_codes[t][:].bitcast(FP8X4),
+                lhsT_scale=w1_scales[t][:],
+                rhs=xw[:, a:b].bitcast(FP8X4),
+                rhs_scale=xs[:, a:b],
+                start=True,
+                stop=True,
+            )
+            nc.scalar.activation(h[t][:, a:b], acc[:], RELU)
+
+        for a, b in WORD_SLICES:
+            nc.vector.tensor_copy(xw[:, a:b], xw_all[:].indirect(offs_t[:, a // LANES : b // LANES]))
+            first_product(0, a, b)
+
+        for t in range(1, TILES):
+            quantize_w1(t)
+            for a in range(0, S, 512):
+                first_product(t, a, a + 512)
+
+        zt = {}
+        for b0, b1 in PIECES:
+            zt[b0] = keep.tile([P, b1 - b0, 2, 2 * P], BF16, name=f"zt{b0}", align_bytes=64)
+        g = keep.tile([P, V], F32, name="g")
+
+        def gather_tile(pieces, t):
+            c0, c1 = pieces[0][0], pieces[-1][1]
+            a, b = c0 * P, c1 * P
+            terms = []
+            for dd in range(D):
+                term = keep.tile([P, b - a], F32, name=f"term{c0}_{t}_{dd}")
+                nc.vector.tensor_tensor(term[:], h[t][:].indirect(pos_t[dd][:, a // LANES : b // LANES]), gate_t[dd][:, a:b], MULT)
+                terms.append(term)
+            sums = psum.tile([P, c1 - c0, P], F32, name="sums", tag="sums", bufs=2)
+            for vb in range(c1 - c0):
+                for dd in range(D):
+                    nc.tensor.matmul(
+                        sums[:, vb, :],
+                        terms[dd][:, vb * P : (vb + 1) * P],
+                        ident[:],
+                        start=(dd == 0),
+                        stop=(dd == D - 1),
+                        is_transpose=True,
+                    )
+            for b0, b1 in pieces:
+                nc.scalar.copy(
+                    zt[b0][:, :, :, 64 * t : 64 * (t + 1)].rearrange("p b u (m e) -> p u b m e", e=2),
+                    sums[:, b0 - c0 : b1 - c0, :].rearrange("p b (m u e) -> p u b m e", u=2, e=2),
+                )
+
+        def second_product(b0, b1):
+            nb = b1 - b0
+            a, b = b0 * P, b1 * P
+            back = psum.tile([P, nb, 2, P], F32, name="back", tag="back", bufs=2)
+            for vb in range(nb):
+                for u in range(2):
+                    nc.tensor.transpose(back[:, vb, u, :], zt[b0][:, vb, u, :].bitcast(F32), ident[:])
+            grouped = keep.tile([P, nb * P * PACK], BF16, name=f"z_grouped{b0}", align_bytes=64)
+            nc.scalar.copy(
+                grouped[:].bitcast(F32).rearrange("p (b v u) -> p b v u", b=nb, u=2),
+                back[:].rearrange("p b u v -> p b v u"),
+            )
+            codes = keep.tile([P, nb * P], U32, name=f"z_codes{b0}", align_bytes=64)
+            scales = keep.tile([P, nb * P], U8, name=f"z_scales{b0}", align_bytes=64)
+            nc.vector.quantize_mx(out=codes[:].bitcast(FP8X4), scales=scales[:], in_=grouped[:])
+            acc = psum.tile([P, nb * P], F32, name="acc", tag="acc", bufs=4)
+            nc.tensor.matmul_mx(
+                out=acc[:],
+                lhsT=w2_w[:].bitcast(FP4X4),
+                lhsT_scale=w2_s[:],
+                rhs=codes[:].bitcast(FP8X4),
+                rhs_scale=scales[:],
+                start=True,
+                stop=True,
+            )
+            if b0 == 0:
+                nc.scalar.activation(g[:, a:b], acc[:], RELU)
+            else:
+                nc.vector.tensor_scalar(g[:, a:b], acc[:], 0.0, None, MAX)
+
+        for t in range(TILES):
+            gather_tile(PIECES[:1], t)
+        second_product(*PIECES[0])
+        for t in range(TILES - 1):
+            gather_tile(PIECES[1:], t)
+        for piece in PIECES[1:]:
+            gather_tile((piece,), TILES - 1)
+            second_product(*piece)
+
+        terms2 = []
+        for dd in range(D):
+            term = keep.tile([P, U], F32, name=f"term2_{dd}")
+            nc.vector.tensor_tensor(term[:], g[:].indirect(nxt_t[dd][:]), gate2_t[:, dd, :], MULT)
+            terms2.append(term)
+        part = keep.tile([P, U], F32, name="part")
+        nc.vector.tensor_tensor(part[:], terms2[0][:], terms2[1][:], ADD)
+        res = keep.tile([P, U], F32, name="res")
+        nc.vector.tensor_tensor(res[:], part[:], terms2[2][:], ADD)
+        nc.sync.dma_start(out, res[:])

@@ -1,3 +1,4 @@
+import math
 from contextlib import ExitStack
 
 import concourse.mybir as mybir
@@ -25,8 +26,7 @@ PACK = 4
 LANES = 16
 TILES = H // P
 WORD_SLICES = ((0, 512), (512, 768), (768, 1024))
-W1_LOADS = ((0, 1), (1, 2), (2, 3), (3, 4))
-PIECES = ((0, 2), (2, 3), (3, 4))
+HALF = H // 2
 
 
 def tile_picked_hop2_relu_p_kernel(
@@ -42,156 +42,173 @@ def tile_picked_hop2_relu_p_kernel(
             nc.sync.dma_start(t[:], ap)
             return t
 
-        w1_rows = w1.rearrange("(p j) c -> p j c", j=PACK)
-        w1_raw = {}
+        late = ctx.enter_context(tc.tile_pool(name="late", bufs=1))
+        late_words = T + PACK * HALF + D * V + D * U
+        zeros = late.tile([P, late_words], I32, name="zeros", offset=0)
+        used = [0]
 
-        def load_w1(t0, t1):
-            raw = keep.tile([P, PACK, (t1 - t0) * P], F32, name=f"w1_raw{t0}")
-            nc.sync.dma_start(raw[:], w1_rows[:, :, t0 * P : t1 * P])
-            for t in range(t0, t1):
-                w1_raw[t] = raw[:, :, (t - t0) * P : (t - t0 + 1) * P]
+        def late_tile(shape, dtype, name):
+            t = late.tile(shape, dtype, name=name, offset=used[0])
+            used[0] = used[0] + 4 * math.prod(shape[1:])
+            return t
+
+        w1_rows = w1.rearrange("(p j) c -> p j c", j=PACK)
 
         xs_all = keep.tile([P, T], U8, name="xs_all", align_bytes=64)
-        nc.vector.memset(xs_all[:].bitcast(I32), 0)
         w2_s = keep.tile([P, N], U8, name="w2_s", align_bytes=64)
-        zeros = keep.tile([P, N // PACK], I32, name="zeros", tag="xw_all", align_bytes=64)
-        nc.vector.memset(zeros[:], 0)
-        nc.vector.tensor_copy(w2_s[:].bitcast(I32), zeros[:])
+        nc.vector.memset(xs_all[:].bitcast(I32), 0)
+        nc.vector.memset(zeros[:, : N // PACK], 0)
+        nc.vector.tensor_copy(w2_s[:].bitcast(I32), zeros[:, : N // PACK])
         ident = keep.tile([P, P], F32, name="ident")
         make_identity(nc, ident[:])
 
         offs_t = load_list(offs, "offs_t")
-        load_w1(*W1_LOADS[0])
+        w1_lo = keep.tile([P, PACK, HALF], F32, name="w1_lo")
+        nc.sync.dma_start(w1_lo[:], w1_rows[:, :, :HALF])
         for q in range(4):
             nc.sync.dma_start(xs_all[32 * q : 32 * q + 4, :].bitcast(I32), x_scales[0, 4 * q : 4 * q + 4, :].bitcast(I32))
-        xw_all = keep.tile([P, T], U32, name="xw_all", tag="xw_all", align_bytes=64)
+        xw_all = late_tile([P, T], U32, "xw_all")
         nc.sync.dma_start(xw_all[:].bitcast(I32), x_words[0].rearrange("p c r -> p (c r)").bitcast(I32))
-        for t0, t1 in W1_LOADS[1:]:
-            load_w1(t0, t1)
-        pos_t = []
+        w1_hi = late_tile([P, PACK, HALF], F32, "w1_hi")
+        nc.sync.dma_start(w1_hi[:], w1_rows[:, :, HALF:])
+        pos_t = [load_list(ap, f"pos_t{dd}") for dd, ap in enumerate((pos1, pos2, pos3))]
         gate_t = []
-        for dd, ap in enumerate((pos1, pos2, pos3)):
-            pos_t.append(load_list(ap, f"pos_t{dd}"))
-            gt = keep.tile([P, V], F32, name=f"gate_t{dd}")
+        for dd in range(D):
+            gt = late_tile([P, V], F32, f"gate_t{dd}")
             nc.sync.dma_start(gt[:], gate[dd])
             gate_t.append(gt)
+        nxt_t = [load_list(ap, f"nxt_t{dd}") for dd, ap in enumerate((nxt1, nxt2, nxt3))]
         w2_w = keep.tile([P, 2 * N], U8, name="w2_w", align_bytes=64)
         nc.sync.dma_start(w2_w[:].bitcast(I32), w2_words[0].bitcast(I32))
         for q in range(4):
             nc.sync.dma_start(w2_s[32 * q : 32 * q + 4, :].bitcast(I32), w2_scales[0, 4 * q : 4 * q + 4, :].bitcast(I32))
-        nxt_t = [load_list(ap, f"nxt_t{dd}") for dd, ap in enumerate((nxt1, nxt2, nxt3))]
-        gate2_t = keep.tile([P, D, U], F32, name="gate2_t")
+        gate2_t = late_tile([P, D, U], F32, "gate2_t")
         nc.sync.dma_start(gate2_t[:], gate2.rearrange("d p r -> p d r"))
 
-        w1_codes = {}
-        w1_scales = {}
+        def channels(raw, first):
+            return raw[:].rearrange("p j (m x) -> p m x j", x=PACK)[:, :, first : first + 2, :]
 
-        def quantize_w1(t):
-            grouped = keep.tile([P, P, PACK], BF16, name=f"w1_grouped{t}", align_bytes=64)
-            nc.scalar.activation(grouped[:], w1_raw[t].rearrange("p j c -> p c j"), COPY)
-            w1_codes[t] = keep.tile([P, P], U32, name=f"w1_codes{t}", align_bytes=64)
-            w1_scales[t] = keep.tile([P, P], U8, name=f"w1_scales{t}", align_bytes=64)
-            nc.vector.quantize_mx(
-                out=w1_codes[t][:].bitcast(FP8X4), scales=w1_scales[t][:], in_=grouped[:].rearrange("p c j -> p (c j)")
-            )
+        def quantize(grouped, width, name):
+            codes = keep.tile([P, width], U32, name=f"{name}_codes", align_bytes=64)
+            scales = keep.tile([P, width], U8, name=f"{name}_scales", align_bytes=64)
+            nc.vector.quantize_mx(out=codes[:].bitcast(FP8X4), scales=scales[:], in_=grouped)
+            return codes, scales
 
         xs = keep.tile([P, S], U8, name="xs", align_bytes=64)
         xw = keep.tile([P, S], U32, name="xw", align_bytes=64)
         nc.vector.tensor_copy(xs[:], xs_all[:].indirect(offs_t[:]))
-        quantize_w1(0)
+
+        w1_q = {}
+        wg23 = keep.tile([P, 2, P, PACK], BF16, name="wg23", align_bytes=64)
+        nc.scalar.activation(wg23[:, :, : P // 2, :].rearrange("p x m j -> p m x j"), channels(w1_lo, 2), COPY)
+        wg0 = keep.tile([P, P // 2, 2, PACK], BF16, name="wg0", align_bytes=64)
+        nc.scalar.activation(wg0[:], channels(w1_lo, 0), COPY)
+        codes, scales = quantize(wg0[:].rearrange("p m x j -> p (m x j)"), P, "w0")
+        w1_q[0] = (codes[:], scales[:])
 
         h = [keep.tile([P, S], F32, name=f"h{t}") for t in range(TILES)]
 
+        def product(width, lhs, lhs_scale, rhs, rhs_scale):
+            acc = psum.tile([P, width], F32, name="acc", tag="acc", bufs=4)
+            nc.tensor.matmul_mx(out=acc[:], lhsT=lhs, lhsT_scale=lhs_scale, rhs=rhs, rhs_scale=rhs_scale, start=True, stop=True)
+            return acc
+
         def first_product(t, a, b):
-            acc = psum.tile([P, b - a], F32, name="acc", tag="acc", bufs=4)
-            nc.tensor.matmul_mx(
-                out=acc[:],
-                lhsT=w1_codes[t][:].bitcast(FP8X4),
-                lhsT_scale=w1_scales[t][:],
-                rhs=xw[:, a:b].bitcast(FP8X4),
-                rhs_scale=xs[:, a:b],
-                start=True,
-                stop=True,
-            )
+            acc = product(b - a, w1_q[t][0].bitcast(FP8X4), w1_q[t][1], xw[:, a:b].bitcast(FP8X4), xs[:, a:b])
             nc.scalar.activation(h[t][:, a:b], acc[:], RELU)
 
         for a, b in WORD_SLICES:
             nc.vector.tensor_copy(xw[:, a:b], xw_all[:].indirect(offs_t[:, a // LANES : b // LANES]))
             first_product(0, a, b)
 
+        wg1 = keep.tile([P, P // 2, 2, PACK], BF16, name="wg1", align_bytes=64)
+        nc.scalar.activation(wg1[:], channels(w1_hi, 0), COPY)
+        nc.vector.tensor_copy(wg23[:, :, P // 2 :, :].rearrange("p x m j -> p m x j"), channels(w1_hi, 2))
+        codes, scales = quantize(wg1[:].rearrange("p m x j -> p (m x j)"), P, "w1")
+        w1_q[1] = (codes[:], scales[:])
+        codes, scales = quantize(wg23[:].rearrange("p x m j -> p (x m j)"), 2 * P, "w23")
+        for x in range(2):
+            w1_q[2 + x] = (codes[:, x * P : (x + 1) * P], scales[:, x * P : (x + 1) * P])
         for t in range(1, TILES):
-            quantize_w1(t)
             for a in range(0, S, 512):
                 first_product(t, a, a + 512)
 
-        zt = {}
-        for b0, b1 in PIECES:
-            zt[b0] = keep.tile([P, b1 - b0, 2, 2 * P], BF16, name=f"zt{b0}", align_bytes=64)
         g = keep.tile([P, V], F32, name="g")
 
-        def gather_tile(pieces, t):
-            c0, c1 = pieces[0][0], pieces[-1][1]
-            a, b = c0 * P, c1 * P
+        def gather_term(dst, t, dd, a, b):
+            nc.vector.tensor_tensor(dst, h[t][:].indirect(pos_t[dd][:, a // LANES : b // LANES]), gate_t[dd][:, a:b], MULT)
+
+        def gather_and_sum(t, b0, b1, sums):
             terms = []
             for dd in range(D):
-                term = keep.tile([P, b - a], F32, name=f"term{c0}_{t}_{dd}")
-                nc.vector.tensor_tensor(term[:], h[t][:].indirect(pos_t[dd][:, a // LANES : b // LANES]), gate_t[dd][:, a:b], MULT)
+                term = keep.tile([P, (b1 - b0) * P], F32, name=f"term{t}_{b0}_{dd}")
+                gather_term(term[:], t, dd, b0 * P, b1 * P)
                 terms.append(term)
-            sums = psum.tile([P, c1 - c0, P], F32, name="sums", tag="sums", bufs=2)
-            for vb in range(c1 - c0):
+            for vb in range(b1 - b0):
                 for dd in range(D):
                     nc.tensor.matmul(
-                        sums[:, vb, :],
-                        terms[dd][:, vb * P : (vb + 1) * P],
-                        ident[:],
-                        start=(dd == 0),
-                        stop=(dd == D - 1),
-                        is_transpose=True,
+                        sums[:, vb, :], terms[dd][:, vb * P : (vb + 1) * P], ident[:], start=(dd == 0), stop=(dd == D - 1), is_transpose=True
                     )
-            for b0, b1 in pieces:
-                nc.scalar.copy(
-                    zt[b0][:, :, :, 64 * t : 64 * (t + 1)].rearrange("p b u (m e) -> p u b m e", e=2),
-                    sums[:, b0 - c0 : b1 - c0, :].rearrange("p b (m u e) -> p u b m e", u=2, e=2),
-                )
 
-        def second_product(b0, b1):
-            nb = b1 - b0
+        def second_product(grouped, b0, b1):
             a, b = b0 * P, b1 * P
-            back = psum.tile([P, nb, 2, P], F32, name="back", tag="back", bufs=2)
-            for vb in range(nb):
-                for u in range(2):
-                    nc.tensor.transpose(back[:, vb, u, :], zt[b0][:, vb, u, :].bitcast(F32), ident[:])
-            grouped = keep.tile([P, nb * P * PACK], BF16, name=f"z_grouped{b0}", align_bytes=64)
-            nc.scalar.copy(
-                grouped[:].bitcast(F32).rearrange("p (b v u) -> p b v u", b=nb, u=2),
-                back[:].rearrange("p b u v -> p b v u"),
-            )
-            codes = keep.tile([P, nb * P], U32, name=f"z_codes{b0}", align_bytes=64)
-            scales = keep.tile([P, nb * P], U8, name=f"z_scales{b0}", align_bytes=64)
-            nc.vector.quantize_mx(out=codes[:].bitcast(FP8X4), scales=scales[:], in_=grouped[:])
-            acc = psum.tile([P, nb * P], F32, name="acc", tag="acc", bufs=4)
-            nc.tensor.matmul_mx(
-                out=acc[:],
-                lhsT=w2_w[:].bitcast(FP4X4),
-                lhsT_scale=w2_s[:],
-                rhs=codes[:].bitcast(FP8X4),
-                rhs_scale=scales[:],
-                start=True,
-                stop=True,
-            )
-            if b0 == 0:
+            codes, scales = quantize(grouped[:].rearrange("p v j -> p (v j)"), b - a, f"z{b0}")
+            acc = product(b - a, w2_w[:].bitcast(FP4X4), w2_s[:], codes[:].bitcast(FP8X4), scales[:])
+            if b1 < V // P:
                 nc.scalar.activation(g[:, a:b], acc[:], RELU)
             else:
                 nc.vector.tensor_scalar(g[:, a:b], acc[:], 0.0, None, MAX)
 
-        for t in range(TILES):
-            gather_tile(PIECES[:1], t)
-        second_product(*PIECES[0])
-        for t in range(TILES - 1):
-            gather_tile(PIECES[1:], t)
-        for piece in PIECES[1:]:
-            gather_tile((piece,), TILES - 1)
-            second_product(*piece)
+        zt_lo = keep.tile([P, V // P, 2, P], BF16, name="zt_lo", align_bytes=64)
+        for t in range(2):
+            sums = psum.tile([P, V // P, P], F32, name="sums", tag="sums", bufs=2)
+            gather_and_sum(t, 0, V // P, sums)
+            nc.scalar.copy(zt_lo[:, :, t, :], sums[:])
+
+        def low_words(vb):
+            return zt_lo[:, vb, :, :].rearrange("p t m -> p (t m)").bitcast(F32)
+
+        def word_pairs(grouped):
+            return grouped[:].rearrange("p v j -> p (v j)").bitcast(F32).rearrange("p (v u) -> p v u", u=2)
+
+        back_a = psum.tile([P, 2, 2, P], F32, name="back_a", tag="back", bufs=2)
+        back_b = psum.tile([P, 2, P], F32, name="back_b", tag="back", bufs=2)
+        grouped_b = [keep.tile([P, P, PACK], BF16, name=f"grouped_b{vb}", align_bytes=64) for vb in range(2)]
+        for vb in range(2):
+            nc.tensor.transpose(back_a[:, vb, 0, :], low_words(vb), ident[:])
+        for vb in range(2):
+            nc.tensor.transpose(back_b[:, vb, :], low_words(2 + vb), ident[:])
+        for vb in range(2):
+            nc.scalar.copy(word_pairs(grouped_b[vb])[:, :, 0], back_b[:, vb, :])
+
+        sums = psum.tile([P, 2, 2, P], F32, name="sums", tag="sums", bufs=2)
+        for x in range(2):
+            gather_and_sum(2 + x, 0, 2, sums[:, x, :, :])
+        zt_hi = keep.tile([P, 2, P, 2], BF16, name="zt_hi", tag="zt_hi", align_bytes=64)
+        nc.scalar.copy(zt_hi[:], sums[:].rearrange("p x b m -> p b m x"))
+        for vb in range(2):
+            nc.tensor.transpose(back_a[:, vb, 1, :], zt_hi[:, vb, :, :].rearrange("p m x -> p (m x)").bitcast(F32), ident[:])
+        grouped_a = keep.tile([P, 2 * P, PACK], BF16, name="grouped_a", align_bytes=64)
+        nc.scalar.copy(word_pairs(grouped_a).rearrange("p (b v) u -> p b v u", b=2), back_a[:].rearrange("p b u v -> p b v u"))
+        second_product(grouped_a, 0, 2)
+
+        last = [keep.tile([P, 2, 2 * P], F32, name=f"last{dd}") for dd in range(2)]
+        for dd in range(2):
+            for x in range(2):
+                gather_term(last[dd][:, x, :], 2 + x, dd, 2 * P, V)
+        pair = keep.tile([P, 2, 2 * P], F32, name="pair")
+        nc.vector.tensor_tensor(pair[:], last[0][:], last[1][:], ADD)
+        third = keep.tile([P, 2, 2 * P], F32, name="third", tag="zt_hi", align_bytes=64)
+        gather_term(third[:, 0, :], 2, 2, 2 * P, V)
+        for vb in range(2):
+            gather_term(third[:, 1, vb * P : (vb + 1) * P], 3, 2, (2 + vb) * P, (3 + vb) * P)
+        for vb in range(2):
+            cols = slice(vb * P, (vb + 1) * P)
+            nc.vector.tensor_tensor(
+                grouped_b[vb][:, :, 2:4], pair[:, :, cols].rearrange("p x v -> p v x"), third[:, :, cols].rearrange("p x v -> p v x"), ADD
+            )
+        for vb in range(2):
+            second_product(grouped_b[vb], 2 + vb, 3 + vb)
 
         terms2 = []
         for dd in range(D):
@@ -199,7 +216,10 @@ def tile_picked_hop2_relu_p_kernel(
             nc.vector.tensor_tensor(term[:], g[:].indirect(nxt_t[dd][:]), gate2_t[:, dd, :], MULT)
             terms2.append(term)
         part = keep.tile([P, U], F32, name="part")
-        nc.vector.tensor_tensor(part[:], terms2[0][:], terms2[1][:], ADD)
         res = keep.tile([P, U], F32, name="res")
-        nc.vector.tensor_tensor(res[:], part[:], terms2[2][:], ADD)
-        nc.sync.dma_start(out, res[:])
+        halves = (slice(0, U // 2), slice(U // 2, U))
+        for cols in halves:
+            nc.vector.tensor_tensor(part[:, cols], terms2[0][:, cols], terms2[1][:, cols], ADD)
+        for cols in halves:
+            nc.vector.tensor_tensor(res[:, cols], part[:, cols], terms2[2][:, cols], ADD)
+            nc.sync.dma_start(out[:, cols], res[:, cols])

@@ -122,7 +122,7 @@ def tile_picked_hop2_relu_p_kernel(
             first_product(0, a, b)
 
         wg1 = keep.tile([P, P // 2, 2, PACK], BF16, name="wg1", align_bytes=64)
-        nc.scalar.activation(wg1[:], channels(w1_hi, 0), COPY)
+        nc.vector.tensor_copy(wg1[:], channels(w1_hi, 0))
         nc.vector.tensor_copy(wg23[:, :, P // 2 :, :].rearrange("p x m j -> p m x j"), channels(w1_hi, 2))
         codes, scales = quantize(wg1[:].rearrange("p m x j -> p (m x j)"), P, "w1")
         w1_q[1] = (codes[:], scales[:])

import math
from contextlib import ExitStack

import concourse.mybir as mybir
from concourse.masks import make_identity

K, T, S, D, V, H, N, U = 512, 2048, 1024, 3, 512, 512, 128, 256
FLOPS = 2 * K * H * S + 2 * H * N * V

F32 = mybir.dt.float32
BF16 = mybir.dt.bfloat16
I32 = mybir.dt.int32
U32 = mybir.dt.uint32
U16 = mybir.dt.uint16
U8 = mybir.dt.uint8
FP8X4 = mybir.dt.float8_e4m3fn_x4
FP4X4 = mybir.dt.float4_e2m1fn_x4
MULT = mybir.AluOpType.mult
ADD = mybir.AluOpType.add
MAX = mybir.AluOpType.max
RELU = mybir.ActivationFunctionType.Relu
COPY = mybir.ActivationFunctionType.Copy

P = 128
PACK = 4
LANES = 16
TILES = H // P
WORD_SLICES = ((0, 512), (512, 768), (768, 1024))
HALF = H // 2


def tile_picked_hop2_relu_p_kernel(
    tc, x_words, x_scales, w1, w2_words, w2_scales, gate, gate2, offs, pos1, pos2, pos3, nxt1, nxt2, nxt3, out
):
    nc = tc.nc
    with ExitStack() as ctx:
        keep = ctx.enter_context(tc.tile_pool(name="keep", bufs=1))
        psum = ctx.enter_context(tc.psum_pool(name="psum", bufs=1))

        def load_list(ap, name):
            t = keep.tile(list(ap.shape), U16, name=name)
            nc.sync.dma_start(t[:], ap)
            return t

        late = ctx.enter_context(tc.tile_pool(name="late", bufs=1))
        late_words = T + PACK * HALF + D * V + D * U
        zeros = late.tile([P, late_words], I32, name="zeros", offset=0)
        used = [0]

        def late_tile(shape, dtype, name):
            t = late.tile(shape, dtype, name=name, offset=used[0])
            used[0] = used[0] + 4 * math.prod(shape[1:])
            return t

        w1_rows = w1.rearrange("(p j) c -> p j c", j=PACK)

        xs_all = keep.tile([P, T], U8, name="xs_all", align_bytes=64)
        w2_s = keep.tile([P, N], U8, name="w2_s", align_bytes=64)
        nc.vector.memset(xs_all[:].bitcast(I32), 0)
        nc.vector.memset(zeros[:, : N // PACK], 0)
        nc.vector.tensor_copy(w2_s[:].bitcast(I32), zeros[:, : N // PACK])
        ident = keep.tile([P, P], F32, name="ident")
        make_identity(nc, ident[:])

        offs_t = load_list(offs, "offs_t")
        w1_lo = keep.tile([P, PACK, HALF], F32, name="w1_lo")
        nc.sync.dma_start(w1_lo[:], w1_rows[:, :, :HALF])
        for q in range(4):
            nc.sync.dma_start(xs_all[32 * q : 32 * q + 4, :].bitcast(I32), x_scales[0, 4 * q : 4 * q + 4, :].bitcast(I32))
        xw_all = late_tile([P, T], U32, "xw_all")
        nc.sync.dma_start(xw_all[:].bitcast(I32), x_words[0].rearrange("p c r -> p (c r)").bitcast(I32))
        w1_hi = late_tile([P, PACK, HALF], F32, "w1_hi")
        nc.sync.dma_start(w1_hi[:], w1_rows[:, :, HALF:])
        pos_t = [load_list(ap, f"pos_t{dd}") for dd, ap in enumerate((pos1, pos2, pos3))]
        gate_t = []
        for dd in range(D):
            gt = late_tile([P, V], F32, f"gate_t{dd}")
            nc.sync.dma_start(gt[:], gate[dd])
            gate_t.append(gt)
        nxt_t = [load_list(ap, f"nxt_t{dd}") for dd, ap in enumerate((nxt1, nxt2, nxt3))]
        w2_w = keep.tile([P, 2 * N], U8, name="w2_w", align_bytes=64)
        nc.sync.dma_start(w2_w[:].bitcast(I32), w2_words[0].bitcast(I32))
        for q in range(4):
            nc.sync.dma_start(w2_s[32 * q : 32 * q + 4, :].bitcast(I32), w2_scales[0, 4 * q : 4 * q + 4, :].bitcast(I32))
        gate2_t = late_tile([P, D, U], F32, "gate2_t")
        nc.sync.dma_start(gate2_t[:], gate2.rearrange("d p r -> p d r"))

        def channels(raw, first):
            return raw[:].rearrange("p j (m x) -> p m x j", x=PACK)[:, :, first : first + 2, :]

        def quantize(grouped, width, name):
            codes = keep.tile([P, width], U32, name=f"{name}_codes", align_bytes=64)
            scales = keep.tile([P, width], U8, name=f"{name}_scales", align_bytes=64)
            nc.vector.quantize_mx(out=codes[:].bitcast(FP8X4), scales=scales[:], in_=grouped)
            return codes, scales

        xs = keep.tile([P, S], U8, name="xs", align_bytes=64)
        xw = keep.tile([P, S], U32, name="xw", align_bytes=64)
        nc.vector.tensor_copy(xs[:], xs_all[:].indirect(offs_t[:]))

        w1_q = {}
        wg23 = keep.tile([P, 2, P, PACK], BF16, name="wg23", align_bytes=64)
        nc.scalar.activation(wg23[:, :, : P // 2, :].rearrange("p x m j -> p m x j"), channels(w1_lo, 2), COPY)
        wg0 = keep.tile([P, P // 2, 2, PACK], BF16, name="wg0", align_bytes=64)
        nc.scalar.activation(wg0[:], channels(w1_lo, 0), COPY)
        codes, scales = quantize(wg0[:].rearrange("p m x j -> p (m x j)"), P, "w0")
        w1_q[0] = (codes[:], scales[:])

        h = [keep.tile([P, S], F32, name=f"h{t}") for t in range(TILES)]

        def product(width, lhs, lhs_scale, rhs, rhs_scale):
            acc = psum.tile([P, width], F32, name="acc", tag="acc", bufs=4)
            nc.tensor.matmul_mx(out=acc[:], lhsT=lhs, lhsT_scale=lhs_scale, rhs=rhs, rhs_scale=rhs_scale, start=True, stop=True)
            return acc

        def first_product(t, a, b):
            acc = product(b - a, w1_q[t][0].bitcast(FP8X4), w1_q[t][1], xw[:, a:b].bitcast(FP8X4), xs[:, a:b])
            nc.scalar.activation(h[t][:, a:b], acc[:], RELU)

        for a, b in WORD_SLICES:
            nc.vector.tensor_copy(xw[:, a:b], xw_all[:].indirect(offs_t[:, a // LANES : b // LANES]))
            first_product(0, a, b)

        wg1 = keep.tile([P, P // 2, 2, PACK], BF16, name="wg1", align_bytes=64)
        nc.vector.tensor_copy(wg1[:], channels(w1_hi, 0))
        nc.vector.tensor_copy(wg23[:, :, P // 2 :, :].rearrange("p x m j -> p m x j"), channels(w1_hi, 2))
        codes, scales = quantize(wg1[:].rearrange("p m x j -> p (m x j)"), P, "w1")
        w1_q[1] = (codes[:], scales[:])
        codes, scales = quantize(wg23[:].rearrange("p x m j -> p (x m j)"), 2 * P, "w23")
        for x in range(2):
            w1_q[2 + x] = (codes[:, x * P : (x + 1) * P], scales[:, x * P : (x + 1) * P])
        for t in range(1, TILES):
            for a in range(0, S, 512):
                first_product(t, a, a + 512)

        g = keep.tile([P, V], F32, name="g")

        def gather_term(dst, t, dd, a, b):
            nc.vector.tensor_tensor(dst, h[t][:].indirect(pos_t[dd][:, a // LANES : b // LANES]), gate_t[dd][:, a:b], MULT)

        def gather_and_sum(t, b0, b1, sums):
            terms = []
            for dd in range(D):
                term = keep.tile([P, (b1 - b0) * P], F32, name=f"term{t}_{b0}_{dd}")
                gather_term(term[:], t, dd, b0 * P, b1 * P)
                terms.append(term)
            for vb in range(b1 - b0):
                for dd in range(D):
                    nc.tensor.matmul(
                        sums[:, vb, :], terms[dd][:, vb * P : (vb + 1) * P], ident[:], start=(dd == 0), stop=(dd == D - 1), is_transpose=True
                    )

        def second_product(grouped, b0, b1):
            a, b = b0 * P, b1 * P
            codes, scales = quantize(grouped[:].rearrange("p v j -> p (v j)"), b - a, f"z{b0}")
            acc = product(b - a, w2_w[:].bitcast(FP4X4), w2_s[:], codes[:].bitcast(FP8X4), scales[:])
            if b1 < V // P:
                nc.scalar.activation(g[:, a:b], acc[:], RELU)
            else:
                nc.vector.tensor_scalar(g[:, a:b], acc[:], 0.0, None, MAX)

        zt_lo = keep.tile([P, V // P, 2, P], BF16, name="zt_lo", align_bytes=64)
        for t in range(2):
            sums = psum.tile([P, V // P, P], F32, name="sums", tag="sums", bufs=2)
            gather_and_sum(t, 0, V // P, sums)
            nc.scalar.copy(zt_lo[:, :, t, :], sums[:])

        def low_words(vb):
            return zt_lo[:, vb, :, :].rearrange("p t m -> p (t m)").bitcast(F32)

        def word_pairs(grouped):
            return grouped[:].rearrange("p v j -> p (v j)").bitcast(F32).rearrange("p (v u) -> p v u", u=2)

        back_a = psum.tile([P, 2, 2, P], F32, name="back_a", tag="back", bufs=2)
        back_b = psum.tile([P, 2, P], F32, name="back_b", tag="back", bufs=2)
        grouped_b = [keep.tile([P, P, PACK], BF16, name=f"grouped_b{vb}", align_bytes=64) for vb in range(2)]
        for vb in range(2):
            nc.tensor.transpose(back_a[:, vb, 0, :], low_words(vb), ident[:])
        for vb in range(2):
            nc.tensor.transpose(back_b[:, vb, :], low_words(2 + vb), ident[:])
        for vb in range(2):
            nc.scalar.copy(word_pairs(grouped_b[vb])[:, :, 0], back_b[:, vb, :])

        sums = psum.tile([P, 2, 2, P], F32, name="sums", tag="sums", bufs=2)
        for x in range(2):
            gather_and_sum(2 + x, 0, 2, sums[:, x, :, :])
        zt_hi = keep.tile([P, 2, P, 2], BF16, name="zt_hi", tag="zt_hi", align_bytes=64)
        nc.scalar.copy(zt_hi[:], sums[:].rearrange("p x b m -> p b m x"))
        for vb in range(2):
            nc.tensor.transpose(back_a[:, vb, 1, :], zt_hi[:, vb, :, :].rearrange("p m x -> p (m x)").bitcast(F32), ident[:])
        grouped_a = keep.tile([P, 2 * P, PACK], BF16, name="grouped_a", align_bytes=64)
        nc.scalar.copy(word_pairs(grouped_a).rearrange("p (b v) u -> p b v u", b=2), back_a[:].rearrange("p b u v -> p b v u"))
        second_product(grouped_a, 0, 2)

        last = [keep.tile([P, 2, 2 * P], F32, name=f"last{dd}") for dd in range(2)]
        for dd in range(2):
            for x in range(2):
                gather_term(last[dd][:, x, :], 2 + x, dd, 2 * P, V)
        pair = keep.tile([P, 2, 2 * P], F32, name="pair")
        nc.vector.tensor_tensor(pair[:], last[0][:], last[1][:], ADD)
        third = keep.tile([P, 2, 2 * P], F32, name="third", tag="zt_hi", align_bytes=64)
        gather_term(third[:, 0, :], 2, 2, 2 * P, V)
        for vb in range(2):
            gather_term(third[:, 1, vb * P : (vb + 1) * P], 3, 2, (2 + vb) * P, (3 + vb) * P)
        for vb in range(2):
            cols = slice(vb * P, (vb + 1) * P)
            nc.vector.tensor_tensor(
                grouped_b[vb][:, :, 2:4], pair[:, :, cols].rearrange("p x v -> p v x"), third[:, :, cols].rearrange("p x v -> p v x"), ADD
            )
        for vb in range(2):
            second_product(grouped_b[vb], 2 + vb, 3 + vb)

        terms2 = []
        for dd in range(D):
            term = keep.tile([P, U], F32, name=f"term2_{dd}")
            nc.vector.tensor_tensor(term[:], g[:].indirect(nxt_t[dd][:]), gate2_t[:, dd, :], MULT)
            terms2.append(term)
        part = keep.tile([P, U], F32, name="part")
        res = keep.tile([P, U], F32, name="res")
        halves = (slice(0, U // 2), slice(U // 2, U))
        for cols in halves:
            nc.vector.tensor_tensor(part[:, cols], terms2[0][:, cols], terms2[1][:, cols], ADD)
        for cols in halves:
            nc.vector.tensor_tensor(res[:, cols], part[:, cols], terms2[2][:, cols], ADD)
            nc.sync.dma_start(out[:, cols], res[:, cols])
